import numpy as np
import ml_dtypes


def mxq(x, axis, fmt="e4m3"):
    dtype, down = {"e4m3": (ml_dtypes.float8_e4m3fn, 7), "e5m2": (ml_dtypes.float8_e5m2, 14)}[fmt]
    v = np.moveaxis(np.asarray(x, np.float32).astype(ml_dtypes.bfloat16).astype(np.float64), axis, -1)
    blocks = v.reshape(v.shape[:-1] + (-1, 32))
    amax = np.abs(blocks).max(-1, keepdims=True)
    byte = np.maximum(np.where(amax > 0, np.frexp(amax)[1] - 1 + 127, 0) - down, 1)
    scale = np.exp2(byte - 127.0)
    codes = (blocks / scale).astype(np.float32).astype(dtype).astype(np.float64)
    return np.moveaxis((codes * scale).reshape(v.shape), -1, axis)


WIDE = False


def mx_kscale(k):
    if not WIDE:
        return np.ones(k)
    levels = np.array([10, -10, 5, -5, 0])
    if k % 512:
        return np.exp2(np.random.permutation(np.resize(levels, k // 32))).repeat(32)
    a = np.empty((k // 512, 16))
    for p in range(k // 512):
        a[p, :8] = np.random.permutation(np.resize(levels, 8))
        for g in range(8):
            far = levels[np.abs(levels - a[p, g]) >= 10]
            a[p, g + 8] = far[np.random.randint(len(far))]
    return np.exp2(a.ravel()).repeat(32)


def f64(x):
    return np.asarray(x).astype(np.float64)


E2M1 = np.array([0.0, 0.5, 1.0, 1.5, 2.0, 3.0, 4.0, 6.0, -0.0, -0.5, -1.0, -1.5, -2.0, -3.0, -4.0, -6.0])


def pack_weight(w, fmt):
    k, n = w.shape
    w = f64(np.asarray(w, np.float32).astype(ml_dtypes.bfloat16)).reshape(k // 32, 32, n)
    amax = np.abs(w).max(1)
    if fmt == "e4m3":
        byte = np.frexp(amax)[1] - 1 + 127 - 7
    else:
        mant, ex = np.frexp(amax / 6.0)
        byte = np.where(mant > 0.5, ex, ex - 1) + 127
    byte = np.clip(np.where(amax > 0, byte, 1), 1, 254)
    scaled = (w * np.exp2(127.0 - byte)[:, None, :]).reshape(k, n).astype(np.float32)
    by_word = np.ascontiguousarray(scaled.reshape(k // 512, 128, 4, n).transpose(0, 1, 3, 2))
    if fmt == "e4m3":
        words = by_word.astype(ml_dtypes.float8_e4m3fn).view(np.uint8)
    else:
        c = by_word.astype(ml_dtypes.float4_e2m1fn).view(np.uint8) & 0xF
        words = (c[..., 0::2] | (c[..., 1::2] << 4)).reshape(k // 512, 128, 2 * n)
    return np.ascontiguousarray(words), np.ascontiguousarray(byte.astype(np.uint8).reshape(k // 512, 16, n))


def unpack_weight(words, scales, fmt):
    g, _, n = scales.shape
    words = np.ascontiguousarray(words).reshape(g, 128, n, -1)
    if fmt == "e4m3":
        vals = words.view(ml_dtypes.float8_e4m3fn).astype(np.float64)
    else:
        nib = np.empty((g, 128, n, 4), np.uint8)
        nib[..., 0::2] = words & 0xF
        nib[..., 1::2] = words >> 4
        vals = E2M1[nib]
    vals = vals * np.repeat(np.exp2(scales.astype(np.float64) - 127.0), 8, axis=1)[..., None]
    return vals.transpose(0, 1, 3, 2).reshape(g * 512, n)


def bf(x):
    return np.asarray(x, np.float32).astype(ml_dtypes.bfloat16)


def planes(Y):
    r, m = Y.shape
    b = f64(bf(Y)).reshape(r // 32, 32, m)
    amax = np.abs(b).max(1)
    byte = np.clip(np.where(amax > 0, np.frexp(amax)[1] - 1 + 127 - 7, 1), 1, 254)
    codes = (b * np.exp2(127.0 - byte)[:, None, :]).reshape(r, m).astype(np.float32).astype(ml_dtypes.float8_e4m3fn).view(np.uint8)
    words = codes.reshape(r // 512, 128, 4, m).transpose(0, 1, 3, 2)
    return np.ascontiguousarray(words), np.ascontiguousarray(byte.astype(np.uint8).reshape(r // 512, 16, m))


K, T, R, N = 1024, 512, 512, 512


def setup_inputs():
    n = np.random.standard_normal
    fk = mx_kscale(K)
    fr = mx_kscale(R)
    xtp = pack_weight(n((K, T)) / fk[:, None], "e2m1")
    wap = pack_weight(n((K, R)) * 1 / np.sqrt(K) * fk[:, None] * fr, "e4m3")
    wcp = pack_weight(n((K, R)) * 1 / np.sqrt(K) * fk[:, None] * fr, "e2m1")
    wbp = pack_weight(n((R, N)) * 1 / np.sqrt(R) / fr[:, None], "e4m3")
    wyp = pack_weight(n((K, N)) * 1 / np.sqrt(K) * fk[:, None], "e2m1")
    return {
        "xt_words": xtp[0],
        "xt_scales": xtp[1],
        "wa_words": wap[0],
        "wa_scales": wap[1],
        "wc_words": wcp[0],
        "wc_scales": wcp[1],
        "wb_words": wbp[0],
        "wb_scales": wbp[1],
        "wy_words": wyp[0],
        "wy_scales": wyp[1],
    }


def reference(xt_words, xt_scales, wa_words, wa_scales, wc_words, wc_scales, wb_words, wb_scales, wy_words, wy_scales):
    xtu = unpack_weight(xt_words, xt_scales, "e2m1")
    wau = unpack_weight(wa_words, wa_scales, "e4m3")
    wcu = unpack_weight(wc_words, wc_scales, "e2m1")
    wbu = unpack_weight(wb_words, wb_scales, "e4m3")
    wyu = unpack_weight(wy_words, wy_scales, "e2m1")
    a = wau.T @ xtu
    b = wcu.T @ xtu
    hid = np.maximum(a, b)
    hidq = mxq(hid, 0, "e4m3")
    y = wbu.T @ hidq + wyu.T @ xtu
    words, scales = planes(y)
    return y, words, scales

@@ -1,0 +1,205 @@
+from contextlib import ExitStack
+
+import concourse.mybir as mybir
+from concourse.masks import make_identity
+
+K, T, R, N = 1024, 512, 512, 512
+FLOPS = 2 * T * (2 * K * R + R * N + K * N)
+
+F32 = mybir.dt.float32
+BF16 = mybir.dt.bfloat16
+I32 = mybir.dt.int32
+U8 = mybir.dt.uint8
+FP8X4 = mybir.dt.float8_e4m3fn_x4
+FP4X4 = mybir.dt.float4_e2m1fn_x4
+
+P = 128
+PACK = 4
+PASSES = K // (P * PACK)
+TILES = T // P
+QUADS = 4
+
+
+def tile_mix_hidden_larger_half_and_skip_pl_kernel(
+    tc, xt_words, xt_scales, wa_words, wa_scales, wc_words, wc_scales,
+    wb_words, wb_scales, wy_words, wy_scales, out_0, out_1, out_2,
+):
+    nc = tc.nc
+    with ExitStack() as ctx:
+        sb = ctx.enter_context(tc.tile_pool(name="sb", bufs=1))
+        ps = ctx.enter_context(tc.psum_pool(name="ps", bufs=1))
+        ctx.enter_context(tc.manual_schedule())
+
+        x_w = sb.tile([P, PASSES, 2 * T], U8, align_bytes=64)
+        c_w = sb.tile([P, PASSES, 2 * R], U8, align_bytes=64)
+        a_w = sb.tile([P, PASSES, R], I32, align_bytes=64)
+        y_w_raw = sb.tile([P, PASSES * 2 * N], U8, align_bytes=64)
+        b_w_raw = sb.tile([P, N], I32, align_bytes=64)
+        x_s = sb.tile([P, PASSES, T], U8, align_bytes=64)
+        c_s = sb.tile([P, PASSES, R], U8, align_bytes=64)
+        a_s = sb.tile([P, PASSES, R], U8, align_bytes=64)
+        yb_s_raw = sb.tile([P, PASSES, N], U8, align_bytes=64)
+        y_w = sb.tile([P, PACK * PASSES * 2 * P], U8, align_bytes=64)
+        b_w = sb.tile([P, PACK * P], I32, align_bytes=64)
+        yb_s = sb.tile([P, PACK * PASSES * P], U8, align_bytes=64)
+        ident = sb.tile([P, P], F32, align_bytes=64)
+        out_s = sb.tile([P, T], U8, align_bytes=64)
+
+        def load_scales(engine, plane, scales, quad, row0=0):
+            passes = scales.shape[0]
+            engine.dma_start(
+                out=plane[32 * quad + row0 : 32 * quad + row0 + 4, 0:passes, :].bitcast(I32),
+                in_=scales[:, 4 * quad : 4 * quad + 4, :].rearrange("z r c -> r z c").bitcast(I32),
+            )
+
+        def load_fp4(tile_view, words):
+            nc.sync.dma_start(out=tile_view.bitcast(I32), in_=words.rearrange("z p c -> p z c").bitcast(I32))
+
+        for plane in (x_s, c_s, a_s, yb_s_raw):
+            nc.vector.memset(plane[:].bitcast(I32), 0)
+        make_identity(nc, ident[:])
+
+        load_fp4(x_w[:], xt_words)
+        for quad in range(QUADS):
+            load_scales(nc.sync, x_s, xt_scales, quad)
+        for quad in range(2):
+            load_scales(nc.sync, c_s, wc_scales, quad)
+        load_fp4(c_w[:], wc_words)
+        for quad in range(2, QUADS):
+            load_scales(nc.sync, c_s, wc_scales, quad)
+        nc.sync.dma_start(out=a_w[:], in_=wa_words.rearrange("z p c r -> p z (c r)").bitcast(I32))
+        for quad in range(QUADS):
+            load_scales(nc.sync, a_s, wa_scales, quad)
+        load_fp4(y_w_raw[:].rearrange("p (z c) -> p z c", z=PASSES), wy_words)
+        for quad in range(QUADS):
+            load_scales(nc.gpsimd, yb_s_raw, wb_scales, quad, row0=4)
+        nc.sync.dma_start(out=b_w_raw[:], in_=wb_words[0].rearrange("p c r -> p (c r)").bitcast(I32))
+        for quad in range(QUADS):
+            load_scales(nc.sync, yb_s_raw, wy_scales, quad)
+
+        def first_layer(bank, tt, w_view, w_scale):
+            for z in range(PASSES):
+                nc.tensor.matmul_mx(
+                    out=bank[:],
+                    lhsT=x_w[:, z, 2 * P * tt : 2 * P * (tt + 1)].bitcast(FP4X4),
+                    lhsT_scale=x_s[:, z, P * tt : P * (tt + 1)],
+                    rhs=w_view(z),
+                    rhs_scale=w_scale[:, z, :],
+                    start=(z == 0),
+                    stop=(z == PASSES - 1),
+                )
+
+        def by_word(bank):
+            return bank[:].rearrange("t (p u e) -> t u p e", u=2, e=2)
+
+        b_sb = []
+        for tt in range(TILES):
+            bank = ps.tile([P, R], F32, name="b%d" % tt, tag="low%d" % tt)
+            first_layer(bank, tt, lambda z: c_w[:, z, :].bitcast(FP4X4), c_s)
+            held = sb.tile([P, R], F32, name="b_sb%d" % tt, align_bytes=64)
+            nc.scalar.copy(out=held[:].rearrange("t (u p e) -> t u p e", u=2, e=2), in_=by_word(bank))
+            b_sb.append(held)
+
+        nc.vector.tensor_copy(
+            out=y_w[:].rearrange("p (j g i b) -> p g j i b", j=PACK, i=8, b=2),
+            in_=y_w_raw[:].rearrange("p (g i j b) -> p g j i b", j=PACK, i=8, b=2),
+        )
+        nc.vector.tensor_copy(
+            out=b_w[:].rearrange("p (j g i) -> p g j i", j=PACK, i=4),
+            in_=b_w_raw[:].rearrange("p (g i j) -> p g j i", j=PACK, i=4),
+        )
+        nc.vector.tensor_copy(
+            out=yb_s[:].rearrange("p (j g i) -> p g j i", j=PACK, i=16),
+            in_=yb_s_raw[:].rearrange("p z (g i j) -> p (z g) j i", j=PACK, i=16),
+        )
+
+        hid_t = []
+        for tt in range(TILES):
+            bank = ps.tile([P, R], F32, name="a%d" % tt, tag="high%d" % tt)
+            first_layer(bank, tt, lambda z: a_w[:, z, :].bitcast(FP8X4), a_s)
+            rounded = sb.tile([P, R], BF16, name="hid_t%d" % tt, align_bytes=64)
+            nc.vector.tensor_tensor(
+                out=rounded[:].rearrange("t (u p e) -> t u p e", u=2, e=2),
+                in0=by_word(bank),
+                in1=b_sb[tt][:].rearrange("t (u p e) -> t u p e", u=2, e=2),
+                op=mybir.AluOpType.max,
+            )
+            hid_t.append(rounded)
+
+        hid_w = {}
+        hid_s = {}
+        y_bank = {}
+
+        def turn(tt):
+            bank = ps.tile([P, 2, P], F32, name="turn%d" % tt, tag="low%d" % tt)
+            words = hid_t[tt][:].bitcast(F32)
+            for u in range(2):
+                nc.tensor.transpose(bank[:, u, :], words[:, P * u : P * (u + 1)], ident[:])
+            grouped = sb.tile([P, PACK * P], BF16, name="grouped%d" % tt, align_bytes=64)
+            nc.scalar.copy(
+                out=grouped[:].bitcast(F32).rearrange("p (t u) -> p t u", u=2),
+                in_=bank[:].rearrange("p u t -> p t u"),
+            )
+            hid_w[tt] = sb.tile([P, P], I32, name="hid_w%d" % tt, align_bytes=64)
+            hid_s[tt] = sb.tile([P, P], U8, name="hid_s%d" % tt, align_bytes=64)
+            nc.vector.quantize_mx(out=hid_w[tt][:].bitcast(FP8X4), scales=hid_s[tt][:], in_=grouped[:])
+
+        def skip(tt):
+            y_bank[tt] = ps.tile([P, PACK, P], F32, name="y%d" % tt, tag="high%d" % tt)
+            for j in range(PACK):
+                for z in range(PASSES):
+                    col = j * PASSES + z
+                    nc.tensor.matmul_mx(
+                        out=y_bank[tt][:, j, :],
+                        lhsT=y_w[:, 2 * P * col : 2 * P * (col + 1)].bitcast(FP4X4),
+                        lhsT_scale=yb_s[:, P * col : P * (col + 1)],
+                        rhs=x_w[:, z, 2 * P * tt : 2 * P * (tt + 1)].bitcast(FP4X4),
+                        rhs_scale=x_s[:, z, P * tt : P * (tt + 1)],
+                        start=(col == 0),
+                        stop=False,
+                    )
+
+        out_rows = out_0.rearrange("(p j) t -> p j t", j=PACK)
+        out_words = out_1[0].rearrange("p c r -> p (c r)").bitcast(I32)
+
+        def second(tt):
+            for j in range(PACK):
+                col = j * PASSES
+                nc.tensor.matmul_mx(
+                    out=y_bank[tt][:, j, :],
+                    lhsT=b_w[:, P * j : P * (j + 1)].bitcast(FP8X4),
+                    lhsT_scale=yb_s[4:P, P * col : P * (col + 1)],
+                    rhs=hid_w[tt][:].bitcast(FP8X4),
+                    rhs_scale=hid_s[tt][:],
+                    start=False,
+                    stop=(j == PACK - 1),
+                )
+            cols = slice(P * tt, P * (tt + 1))
+            result = sb.tile([P, PACK, P], F32, name="result%d" % tt, align_bytes=64)
+            nc.scalar.copy(out=result[:], in_=y_bank[tt][:])
+            nc.sync.dma_start(out=out_rows[:, :, cols], in_=result[:])
+            rounded = sb.tile([P, PACK * P], BF16, name="rounded%d" % tt, align_bytes=64)
+            nc.vector.tensor_copy(
+                out=rounded[:].rearrange("p (g i j) -> p g j i", j=PACK, i=4),
+                in_=result[:].rearrange("p j (g i) -> p g j i", i=4),
+            )
+            codes = sb.tile([P, P], I32, name="codes%d" % tt, align_bytes=64)
+            nc.vector.quantize_mx(out=codes[:].bitcast(FP8X4), scales=out_s[:, cols], in_=rounded[:])
+            nc.sync.dma_start(out=out_words[:, cols], in_=codes[:])
+
+        turn(0)
+        turn(1)
+        turn(2)
+        skip(0)
+        turn(3)
+        second(0)
+        for tt in range(1, TILES):
+            skip(tt)
+            second(tt)
+
+        for quad in range(QUADS):
+            engine = nc.scalar if quad % 2 else nc.sync
+            engine.dma_start(
+                out=out_2[0, 4 * quad : 4 * quad + 4, :].bitcast(I32),
+                in_=out_s[32 * quad : 32 * quad + 4, :].bitcast(I32),
+            )

@@ -18,6 +18,7 @@ PACK = 4
 PASSES = K // (P * PACK)
 TILES = T // P
 QUADS = 4
+WARM_PASSES = 17
 
 
 def tile_mix_hidden_larger_half_and_skip_pl_kernel(
@@ -46,18 +47,30 @@ def tile_mix_hidden_larger_half_and_skip_pl_kernel(
         out_s = sb.tile([P, T], U8, align_bytes=64)
 
         def load_scales(engine, plane, scales, quad, row0=0):
-            passes = scales.shape[0]
+            first = PASSES - scales.shape[0]
             engine.dma_start(
-                out=plane[32 * quad + row0 : 32 * quad + row0 + 4, 0:passes, :].bitcast(I32),
+                out=plane[32 * quad + row0 : 32 * quad + row0 + 4, first:PASSES, :].bitcast(I32),
                 in_=scales[:, 4 * quad : 4 * quad + 4, :].rearrange("z r c -> r z c").bitcast(I32),
             )
 
         def load_fp4(tile_view, words):
             nc.sync.dma_start(out=tile_view.bitcast(I32), in_=words.rearrange("z p c -> p z c").bitcast(I32))
 
-        for plane in (x_s, c_s, a_s, yb_s_raw):
-            nc.vector.memset(plane[:].bitcast(I32), 0)
-        make_identity(nc, ident[:])
+        warm_in = sb.tile([P, PACK * P], BF16, align_bytes=64)
+        warm_w = sb.tile([P, P], I32, align_bytes=64)
+        warm_s = sb.tile([P, P], U8, align_bytes=64)
+        nc.vector.memset(x_s[:].bitcast(I32), 0)
+        nc.vector.memset(yb_s_raw[:].bitcast(I32), 0)
+        nc.vector.memset(warm_in[:], 0.0)
+        nc.vector.memset(c_s[:].bitcast(I32), 0)
+        nc.vector.quantize_mx(out=warm_w[:].bitcast(FP8X4), scales=warm_s[:], in_=warm_in[:])
+        nc.vector.memset(a_s[:].bitcast(I32), 0)
+        warm_bank = ps.tile([P, P], F32, tag="high3")
+        for step in range(WARM_PASSES):
+            nc.tensor.matmul_mx(
+                out=warm_bank[:], lhsT=warm_w[:].bitcast(FP8X4), lhsT_scale=warm_s[:],
+                rhs=warm_w[:].bitcast(FP8X4), rhs_scale=warm_s[:], start=True, stop=True,
+            )
 
         load_fp4(x_w[:], xt_words)
         for quad in range(QUADS):
@@ -67,15 +80,17 @@ def tile_mix_hidden_larger_half_and_skip_pl_kernel(
         load_fp4(c_w[:], wc_words)
         for quad in range(2, QUADS):
             load_scales(nc.sync, c_s, wc_scales, quad)
+        load_fp4(y_w_raw[:].rearrange("p (z c) -> p z c", z=PASSES), wy_words)
         nc.sync.dma_start(out=a_w[:], in_=wa_words.rearrange("z p c r -> p z (c r)").bitcast(I32))
         for quad in range(QUADS):
             load_scales(nc.sync, a_s, wa_scales, quad)
-        load_fp4(y_w_raw[:].rearrange("p (z c) -> p z c", z=PASSES), wy_words)
+        load_scales(nc.sync, yb_s_raw, wy_scales, QUADS - 1)
         for quad in range(QUADS):
-            load_scales(nc.gpsimd, yb_s_raw, wb_scales, quad, row0=4)
+            load_scales(nc.sync, yb_s_raw, wb_scales, quad, row0=4)
         nc.sync.dma_start(out=b_w_raw[:], in_=wb_words[0].rearrange("p c r -> p (c r)").bitcast(I32))
-        for quad in range(QUADS):
-            load_scales(nc.sync, yb_s_raw, wy_scales, quad)
+        for quad in range(QUADS - 1):
+            load_scales(nc.gpsimd, yb_s_raw, wy_scales, quad)
+        make_identity(nc, ident[:])
 
         def first_layer(bank, tt, w_view, w_scale):
             for z in range(PASSES):
@@ -104,101 +119,154 @@ def tile_mix_hidden_larger_half_and_skip_pl_kernel(
             out=y_w[:].rearrange("p (j g i b) -> p g j i b", j=PACK, i=8, b=2),
             in_=y_w_raw[:].rearrange("p (g i j b) -> p g j i b", j=PACK, i=8, b=2),
         )
-        nc.vector.tensor_copy(
-            out=b_w[:].rearrange("p (j g i) -> p g j i", j=PACK, i=4),
-            in_=b_w_raw[:].rearrange("p (g i j) -> p g j i", j=PACK, i=4),
-        )
-        nc.vector.tensor_copy(
-            out=yb_s[:].rearrange("p (j g i) -> p g j i", j=PACK, i=16),
-            in_=yb_s_raw[:].rearrange("p z (g i j) -> p (z g) j i", j=PACK, i=16),
-        )
+        def deal_scales(z):
+            nc.vector.tensor_copy(
+                out=yb_s[:].rearrange("p (j z g i) -> p z g j i", j=PACK, z=PASSES, i=16)[:, z],
+                in_=yb_s_raw[:, z, :].rearrange("p (g i j) -> p g j i", j=PACK, i=16),
+            )
 
-        hid_t = []
-        for tt in range(TILES):
+        deal_scales(0)
+
+        hid_t = {}
+        grouped = {}
+        hid_w = {}
+        hid_s = {}
+        result = {}
+        rounded = {}
+        out_rows = out_0.rearrange("(p j) t -> p j t", j=PACK)
+        out_words = out_1[0].rearrange("p c r -> p (c r)").bitcast(I32)
+
+        def larger(tt):
             bank = ps.tile([P, R], F32, name="a%d" % tt, tag="high%d" % tt)
             first_layer(bank, tt, lambda z: a_w[:, z, :].bitcast(FP8X4), a_s)
-            rounded = sb.tile([P, R], BF16, name="hid_t%d" % tt, align_bytes=64)
+            hid_t[tt] = sb.tile([P, R], BF16, name="hid_t%d" % tt, align_bytes=64)
             nc.vector.tensor_tensor(
-                out=rounded[:].rearrange("t (u p e) -> t u p e", u=2, e=2),
+                out=hid_t[tt][:].rearrange("t (u p e) -> t u p e", u=2, e=2),
                 in0=by_word(bank),
                 in1=b_sb[tt][:].rearrange("t (u p e) -> t u p e", u=2, e=2),
                 op=mybir.AluOpType.max,
             )
-            hid_t.append(rounded)
 
-        hid_w = {}
-        hid_s = {}
-        y_bank = {}
+        def deal_b():
+            nc.vector.tensor_copy(
+                out=b_w[:].rearrange("p (j g i) -> p g j i", j=PACK, i=4),
+                in_=b_w_raw[:].rearrange("p (g i j) -> p g j i", j=PACK, i=4),
+            )
 
         def turn(tt):
             bank = ps.tile([P, 2, P], F32, name="turn%d" % tt, tag="low%d" % tt)
             words = hid_t[tt][:].bitcast(F32)
             for u in range(2):
                 nc.tensor.transpose(bank[:, u, :], words[:, P * u : P * (u + 1)], ident[:])
-            grouped = sb.tile([P, PACK * P], BF16, name="grouped%d" % tt, align_bytes=64)
+            grouped[tt] = sb.tile([P, PACK * P], BF16, name="grouped%d" % tt, align_bytes=64)
             nc.scalar.copy(
-                out=grouped[:].bitcast(F32).rearrange("p (t u) -> p t u", u=2),
+                out=grouped[tt][:].bitcast(F32).rearrange("p (t u) -> p t u", u=2),
                 in_=bank[:].rearrange("p u t -> p t u"),
             )
+
+        def quantize_hid(tt):
             hid_w[tt] = sb.tile([P, P], I32, name="hid_w%d" % tt, align_bytes=64)
             hid_s[tt] = sb.tile([P, P], U8, name="hid_s%d" % tt, align_bytes=64)
-            nc.vector.quantize_mx(out=hid_w[tt][:].bitcast(FP8X4), scales=hid_s[tt][:], in_=grouped[:])
+            nc.vector.quantize_mx(out=hid_w[tt][:].bitcast(FP8X4), scales=hid_s[tt][:], in_=grouped[tt][:])
 
-        def skip(tt):
-            y_bank[tt] = ps.tile([P, PACK, P], F32, name="y%d" % tt, tag="high%d" % tt)
-            for j in range(PACK):
+        def skip_passes(bank, tt, rows):
+            for slot, j in enumerate(rows):
                 for z in range(PASSES):
                     col = j * PASSES + z
                     nc.tensor.matmul_mx(
-                        out=y_bank[tt][:, j, :],
+                        out=bank[:, slot, :],
                         lhsT=y_w[:, 2 * P * col : 2 * P * (col + 1)].bitcast(FP4X4),
                         lhsT_scale=yb_s[:, P * col : P * (col + 1)],
                         rhs=x_w[:, z, 2 * P * tt : 2 * P * (tt + 1)].bitcast(FP4X4),
                         rhs_scale=x_s[:, z, P * tt : P * (tt + 1)],
-                        start=(col == 0),
+                        start=(slot == 0 and z == 0),
                         stop=False,
                     )
 
-        out_rows = out_0.rearrange("(p j) t -> p j t", j=PACK)
-        out_words = out_1[0].rearrange("p c r -> p (c r)").bitcast(I32)
-
-        def second(tt):
-            for j in range(PACK):
-                col = j * PASSES
+        def second_passes(bank, tt, rows):
+            for slot, j in enumerate(rows):
+                col = j * PASSES + PASSES - 1
                 nc.tensor.matmul_mx(
-                    out=y_bank[tt][:, j, :],
+                    out=bank[:, slot, :],
                     lhsT=b_w[:, P * j : P * (j + 1)].bitcast(FP8X4),
                     lhsT_scale=yb_s[4:P, P * col : P * (col + 1)],
                     rhs=hid_w[tt][:].bitcast(FP8X4),
                     rhs_scale=hid_s[tt][:],
                     start=False,
-                    stop=(j == PACK - 1),
+                    stop=(slot == len(rows) - 1),
                 )
-            cols = slice(P * tt, P * (tt + 1))
-            result = sb.tile([P, PACK, P], F32, name="result%d" % tt, align_bytes=64)
-            nc.scalar.copy(out=result[:], in_=y_bank[tt][:])
-            nc.sync.dma_start(out=out_rows[:, :, cols], in_=result[:])
-            rounded = sb.tile([P, PACK * P], BF16, name="rounded%d" % tt, align_bytes=64)
-            nc.vector.tensor_copy(
-                out=rounded[:].rearrange("p (g i j) -> p g j i", j=PACK, i=4),
-                in_=result[:].rearrange("p j (g i) -> p g j i", i=4),
-            )
-            codes = sb.tile([P, P], I32, name="codes%d" % tt, align_bytes=64)
-            nc.vector.quantize_mx(out=codes[:].bitcast(FP8X4), scales=out_s[:, cols], in_=rounded[:])
-            nc.sync.dma_start(out=out_words[:, cols], in_=codes[:])
+            nc.scalar.copy(out=result[tt][:, rows.start : rows.stop, :], in_=bank[:])
+            stored = PACK if tt == TILES - 1 else 2
+            if rows.stop % stored == 0:
+                pair = slice(rows.stop - stored, rows.stop)
+                nc.sync.dma_start(out=out_rows[:, pair, P * tt : P * (tt + 1)], in_=result[tt][:, pair, :])
 
+        def output(tt, tags, skips_first=False):
+            per_bank = PACK // len(tags)
+            result[tt] = sb.tile([P, PACK, P], F32, name="result%d" % tt, align_bytes=64)
+            parts = []
+            for number, tag in enumerate(tags):
+                bank = ps.tile([P, per_bank, P], F32, name="y%d_%d" % (tt, number), tag=tag)
+                rows = range(per_bank * number, per_bank * (number + 1))
+                skip_passes(bank, tt, rows)
+                if skips_first:
+                    parts.append((bank, rows))
+                else:
+                    second_passes(bank, tt, rows)
+            for bank, rows in parts:
+                second_passes(bank, tt, rows)
+
+        def round_result(tt, parts):
+            width = P // parts
+            rounded[tt] = []
+            for part in range(parts):
+                piece = sb.tile([P, PACK * width], BF16, name="rounded%d_%d" % (tt, part), align_bytes=64)
+                nc.vector.tensor_copy(
+                    out=piece[:].rearrange("p (g i j) -> p g j i", j=PACK, i=4),
+                    in_=result[tt][:, :, width * part : width * (part + 1)].rearrange("p j (g i) -> p g j i", i=4),
+                )
+                rounded[tt].append(piece)
+
+        def hand_on(tt):
+            width = P // len(rounded[tt])
+            codes = sb.tile([P, P], I32, name="codes%d" % tt, align_bytes=64)
+            for part, piece in enumerate(rounded[tt]):
+                nc.vector.quantize_mx(
+                    out=codes[:, width * part : width * (part + 1)].bitcast(FP8X4),
+                    scales=out_s[:, P * tt + width * part : P * tt + width * (part + 1)],
+                    in_=piece[:],
+                )
+            nc.sync.dma_start(out=out_words[:, P * tt : P * (tt + 1)], in_=codes[:])
+
+        larger(0)
+        larger(1)
+        larger(2)
         turn(0)
         turn(1)
+        deal_scales(1)
+        deal_b()
+        quantize_hid(0)
+        quantize_hid(1)
+        larger(3)
+        output(0, ["high0", "high1"], skips_first=True)
+        round_result(0, 1)
+        output(1, ["high2", "low0"])
+        hand_on(0)
         turn(2)
-        skip(0)
         turn(3)
-        second(0)
-        for tt in range(1, TILES):
-            skip(tt)
-            second(tt)
+        round_result(1, 1)
+        quantize_hid(2)
+        hand_on(1)
+        quantize_hid(3)
+        output(2, ["high3", "low1"], skips_first=True)
+        round_result(2, 1)
+        hand_on(2)
+        output(3, ["high0", "high1", "high2", "low0"])
+        round_result(3, 2)
+        hand_on(3)
 
         for quad in range(QUADS):
-            engine = nc.scalar if quad % 2 else nc.sync
+            engine = nc.sync if quad == 3 else nc.scalar
             engine.dma_start(
                 out=out_2[0, 4 * quad : 4 * quad + 4, :].bitcast(I32),
                 in_=out_s[32 * quad : 32 * quad + 4, :].bitcast(I32),

@@ -18,7 +18,7 @@ PACK = 4
 PASSES = K // (P * PACK)
 TILES = T // P
 QUADS = 4
-WARM_PASSES = 17
+WARM_PASSES = 18
 
 
 def tile_mix_hidden_larger_half_and_skip_pl_kernel(
@@ -45,6 +45,7 @@ def tile_mix_hidden_larger_half_and_skip_pl_kernel(
         yb_s = sb.tile([P, PACK * PASSES * P], U8, align_bytes=64)
         ident = sb.tile([P, P], F32, align_bytes=64)
         out_s = sb.tile([P, T], U8, align_bytes=64)
+        out_w = sb.tile([P, T], I32, align_bytes=64)
 
         def load_scales(engine, plane, scales, quad, row0=0):
             first = PASSES - scales.shape[0]
@@ -75,15 +76,15 @@ def tile_mix_hidden_larger_half_and_skip_pl_kernel(
         load_fp4(x_w[:], xt_words)
         for quad in range(QUADS):
             load_scales(nc.sync, x_s, xt_scales, quad)
-        for quad in range(2):
-            load_scales(nc.sync, c_s, wc_scales, quad)
+        load_scales(nc.sync, c_s, wc_scales, 0)
         load_fp4(c_w[:], wc_words)
-        for quad in range(2, QUADS):
-            load_scales(nc.sync, c_s, wc_scales, quad)
         load_fp4(y_w_raw[:].rearrange("p (z c) -> p z c", z=PASSES), wy_words)
-        nc.sync.dma_start(out=a_w[:], in_=wa_words.rearrange("z p c r -> p z (c r)").bitcast(I32))
-        for quad in range(QUADS):
+        for quad in range(1, QUADS):
+            load_scales(nc.sync, c_s, wc_scales, quad)
+        for quad in range(QUADS - 1):
             load_scales(nc.sync, a_s, wa_scales, quad)
+        nc.sync.dma_start(out=a_w[:], in_=wa_words.rearrange("z p c r -> p z (c r)").bitcast(I32))
+        load_scales(nc.sync, a_s, wa_scales, QUADS - 1)
         load_scales(nc.sync, yb_s_raw, wy_scales, QUADS - 1)
         for quad in range(QUADS):
             load_scales(nc.sync, yb_s_raw, wb_scales, quad, row0=4)
@@ -126,6 +127,7 @@ def tile_mix_hidden_larger_half_and_skip_pl_kernel(
             )
 
         deal_scales(0)
+        deal_scales(1)
 
         hid_t = {}
         grouped = {}
@@ -229,39 +231,39 @@ def tile_mix_hidden_larger_half_and_skip_pl_kernel(
 
         def hand_on(tt):
             width = P // len(rounded[tt])
-            codes = sb.tile([P, P], I32, name="codes%d" % tt, align_bytes=64)
             for part, piece in enumerate(rounded[tt]):
                 nc.vector.quantize_mx(
-                    out=codes[:, width * part : width * (part + 1)].bitcast(FP8X4),
+                    out=out_w[:, P * tt + width * part : P * tt + width * (part + 1)].bitcast(FP8X4),
                     scales=out_s[:, P * tt + width * part : P * tt + width * (part + 1)],
                     in_=piece[:],
                 )
-            nc.sync.dma_start(out=out_words[:, P * tt : P * (tt + 1)], in_=codes[:])
+            if tt % 2:
+                pair = slice(P * (tt - 1), P * (tt + 1))
+                nc.sync.dma_start(out=out_words[:, pair], in_=out_w[:, pair])
 
         larger(0)
         larger(1)
         larger(2)
         turn(0)
         turn(1)
-        deal_scales(1)
         deal_b()
         quantize_hid(0)
         quantize_hid(1)
         larger(3)
         output(0, ["high0", "high1"], skips_first=True)
-        round_result(0, 1)
-        output(1, ["high2", "low0"])
-        hand_on(0)
         turn(2)
         turn(3)
-        round_result(1, 1)
+        round_result(0, 1)
         quantize_hid(2)
-        hand_on(1)
+        hand_on(0)
         quantize_hid(3)
-        output(2, ["high3", "low1"], skips_first=True)
+        output(1, ["high2", "low0"])
+        round_result(1, 1)
+        hand_on(1)
+        output(2, ["high3", "low1"])
         round_result(2, 1)
         hand_on(2)
-        output(3, ["high0", "high1", "high2", "low0"])
+        output(3, ["high0", "high1", "low2", "low3"])
         round_result(3, 2)
         hand_on(3)
 

from contextlib import ExitStack

import concourse.mybir as mybir
from concourse.masks import make_identity

K, T, R, N = 1024, 512, 512, 512
FLOPS = 2 * T * (2 * K * R + R * N + K * N)

F32 = mybir.dt.float32
BF16 = mybir.dt.bfloat16
I32 = mybir.dt.int32
U8 = mybir.dt.uint8
FP8X4 = mybir.dt.float8_e4m3fn_x4
FP4X4 = mybir.dt.float4_e2m1fn_x4

P = 128
PACK = 4
PASSES = K // (P * PACK)
TILES = T // P
QUADS = 4
WARM_PASSES = 18


def tile_mix_hidden_larger_half_and_skip_pl_kernel(
    tc, xt_words, xt_scales, wa_words, wa_scales, wc_words, wc_scales,
    wb_words, wb_scales, wy_words, wy_scales, out_0, out_1, out_2,
):
    nc = tc.nc
    with ExitStack() as ctx:
        sb = ctx.enter_context(tc.tile_pool(name="sb", bufs=1))
        ps = ctx.enter_context(tc.psum_pool(name="ps", bufs=1))
        ctx.enter_context(tc.manual_schedule())

        x_w = sb.tile([P, PASSES, 2 * T], U8, align_bytes=64)
        c_w = sb.tile([P, PASSES, 2 * R], U8, align_bytes=64)
        a_w = sb.tile([P, PASSES, R], I32, align_bytes=64)
        y_w_raw = sb.tile([P, PASSES * 2 * N], U8, align_bytes=64)
        b_w_raw = sb.tile([P, N], I32, align_bytes=64)
        x_s = sb.tile([P, PASSES, T], U8, align_bytes=64)
        c_s = sb.tile([P, PASSES, R], U8, align_bytes=64)
        a_s = sb.tile([P, PASSES, R], U8, align_bytes=64)
        yb_s_raw = sb.tile([P, PASSES, N], U8, align_bytes=64)
        y_w = sb.tile([P, PACK * PASSES * 2 * P], U8, align_bytes=64)
        b_w = sb.tile([P, PACK * P], I32, align_bytes=64)
        yb_s = sb.tile([P, PACK * PASSES * P], U8, align_bytes=64)
        ident = sb.tile([P, P], F32, align_bytes=64)
        out_s = sb.tile([P, T], U8, align_bytes=64)
        out_w = sb.tile([P, T], I32, align_bytes=64)

        def load_scales(engine, plane, scales, quad, row0=0):
            first = PASSES - scales.shape[0]
            engine.dma_start(
                out=plane[32 * quad + row0 : 32 * quad + row0 + 4, first:PASSES, :].bitcast(I32),
                in_=scales[:, 4 * quad : 4 * quad + 4, :].rearrange("z r c -> r z c").bitcast(I32),
            )

        def load_fp4(tile_view, words):
            nc.sync.dma_start(out=tile_view.bitcast(I32), in_=words.rearrange("z p c -> p z c").bitcast(I32))

        warm_in = sb.tile([P, PACK * P], BF16, align_bytes=64)
        warm_w = sb.tile([P, P], I32, align_bytes=64)
        warm_s = sb.tile([P, P], U8, align_bytes=64)
        nc.vector.memset(x_s[:].bitcast(I32), 0)
        nc.vector.memset(yb_s_raw[:].bitcast(I32), 0)
        nc.vector.memset(warm_in[:], 0.0)
        nc.vector.memset(c_s[:].bitcast(I32), 0)
        nc.vector.quantize_mx(out=warm_w[:].bitcast(FP8X4), scales=warm_s[:], in_=warm_in[:])
        nc.vector.memset(a_s[:].bitcast(I32), 0)
        warm_bank = ps.tile([P, P], F32, tag="high3")
        for step in range(WARM_PASSES):
            nc.tensor.matmul_mx(
                out=warm_bank[:], lhsT=warm_w[:].bitcast(FP8X4), lhsT_scale=warm_s[:],
                rhs=warm_w[:].bitcast(FP8X4), rhs_scale=warm_s[:], start=True, stop=True,
            )

        load_fp4(x_w[:], xt_words)
        for quad in range(QUADS):
            load_scales(nc.sync, x_s, xt_scales, quad)
        load_scales(nc.sync, c_s, wc_scales, 0)
        load_fp4(c_w[:], wc_words)
        load_fp4(y_w_raw[:].rearrange("p (z c) -> p z c", z=PASSES), wy_words)
        for quad in range(1, QUADS):
            load_scales(nc.sync, c_s, wc_scales, quad)
        for quad in range(QUADS - 1):
            load_scales(nc.sync, a_s, wa_scales, quad)
        nc.sync.dma_start(out=a_w[:], in_=wa_words.rearrange("z p c r -> p z (c r)").bitcast(I32))
        load_scales(nc.sync, a_s, wa_scales, QUADS - 1)
        load_scales(nc.sync, yb_s_raw, wy_scales, QUADS - 1)
        for quad in range(QUADS):
            load_scales(nc.sync, yb_s_raw, wb_scales, quad, row0=4)
        nc.sync.dma_start(out=b_w_raw[:], in_=wb_words[0].rearrange("p c r -> p (c r)").bitcast(I32))
        for quad in range(QUADS - 1):
            load_scales(nc.gpsimd, yb_s_raw, wy_scales, quad)
        make_identity(nc, ident[:])

        def first_layer(bank, tt, w_view, w_scale):
            for z in range(PASSES):
                nc.tensor.matmul_mx(
                    out=bank[:],
                    lhsT=x_w[:, z, 2 * P * tt : 2 * P * (tt + 1)].bitcast(FP4X4),
                    lhsT_scale=x_s[:, z, P * tt : P * (tt + 1)],
                    rhs=w_view(z),
                    rhs_scale=w_scale[:, z, :],
                    start=(z == 0),
                    stop=(z == PASSES - 1),
                )

        def by_word(bank):
            return bank[:].rearrange("t (p u e) -> t u p e", u=2, e=2)

        b_sb = []
        for tt in range(TILES):
            bank = ps.tile([P, R], F32, name="b%d" % tt, tag="low%d" % tt)
            first_layer(bank, tt, lambda z: c_w[:, z, :].bitcast(FP4X4), c_s)
            held = sb.tile([P, R], F32, name="b_sb%d" % tt, align_bytes=64)
            nc.scalar.copy(out=held[:].rearrange("t (u p e) -> t u p e", u=2, e=2), in_=by_word(bank))
            b_sb.append(held)

        nc.vector.tensor_copy(
            out=y_w[:].rearrange("p (j g i b) -> p g j i b", j=PACK, i=8, b=2),
            in_=y_w_raw[:].rearrange("p (g i j b) -> p g j i b", j=PACK, i=8, b=2),
        )
        def deal_scales(z):
            nc.vector.tensor_copy(
                out=yb_s[:].rearrange("p (j z g i) -> p z g j i", j=PACK, z=PASSES, i=16)[:, z],
                in_=yb_s_raw[:, z, :].rearrange("p (g i j) -> p g j i", j=PACK, i=16),
            )

        deal_scales(0)
        deal_scales(1)

        hid_t = {}
        grouped = {}
        hid_w = {}
        hid_s = {}
        result = {}
        rounded = {}
        out_rows = out_0.rearrange("(p j) t -> p j t", j=PACK)
        out_words = out_1[0].rearrange("p c r -> p (c r)").bitcast(I32)

        def larger(tt):
            bank = ps.tile([P, R], F32, name="a%d" % tt, tag="high%d" % tt)
            first_layer(bank, tt, lambda z: a_w[:, z, :].bitcast(FP8X4), a_s)
            hid_t[tt] = sb.tile([P, R], BF16, name="hid_t%d" % tt, align_bytes=64)
            nc.vector.tensor_tensor(
                out=hid_t[tt][:].rearrange("t (u p e) -> t u p e", u=2, e=2),
                in0=by_word(bank),
                in1=b_sb[tt][:].rearrange("t (u p e) -> t u p e", u=2, e=2),
                op=mybir.AluOpType.max,
            )

        def deal_b():
            nc.vector.tensor_copy(
                out=b_w[:].rearrange("p (j g i) -> p g j i", j=PACK, i=4),
                in_=b_w_raw[:].rearrange("p (g i j) -> p g j i", j=PACK, i=4),
            )

        def turn(tt):
            bank = ps.tile([P, 2, P], F32, name="turn%d" % tt, tag="low%d" % tt)
            words = hid_t[tt][:].bitcast(F32)
            for u in range(2):
                nc.tensor.transpose(bank[:, u, :], words[:, P * u : P * (u + 1)], ident[:])
            grouped[tt] = sb.tile([P, PACK * P], BF16, name="grouped%d" % tt, align_bytes=64)
            nc.scalar.copy(
                out=grouped[tt][:].bitcast(F32).rearrange("p (t u) -> p t u", u=2),
                in_=bank[:].rearrange("p u t -> p t u"),
            )

        def quantize_hid(tt):
            hid_w[tt] = sb.tile([P, P], I32, name="hid_w%d" % tt, align_bytes=64)
            hid_s[tt] = sb.tile([P, P], U8, name="hid_s%d" % tt, align_bytes=64)
            nc.vector.quantize_mx(out=hid_w[tt][:].bitcast(FP8X4), scales=hid_s[tt][:], in_=grouped[tt][:])

        def skip_passes(bank, tt, rows):
            for slot, j in enumerate(rows):
                for z in range(PASSES):
                    col = j * PASSES + z
                    nc.tensor.matmul_mx(
                        out=bank[:, slot, :],
                        lhsT=y_w[:, 2 * P * col : 2 * P * (col + 1)].bitcast(FP4X4),
                        lhsT_scale=yb_s[:, P * col : P * (col + 1)],
                        rhs=x_w[:, z, 2 * P * tt : 2 * P * (tt + 1)].bitcast(FP4X4),
                        rhs_scale=x_s[:, z, P * tt : P * (tt + 1)],
                        start=(slot == 0 and z == 0),
                        stop=False,
                    )

        def second_passes(bank, tt, rows):
            for slot, j in enumerate(rows):
                col = j * PASSES + PASSES - 1
                nc.tensor.matmul_mx(
                    out=bank[:, slot, :],
                    lhsT=b_w[:, P * j : P * (j + 1)].bitcast(FP8X4),
                    lhsT_scale=yb_s[4:P, P * col : P * (col + 1)],
                    rhs=hid_w[tt][:].bitcast(FP8X4),
                    rhs_scale=hid_s[tt][:],
                    start=False,
                    stop=(slot == len(rows) - 1),
                )
            nc.scalar.copy(out=result[tt][:, rows.start : rows.stop, :], in_=bank[:])
            stored = PACK if tt == TILES - 1 else 2
            if rows.stop % stored == 0:
                pair = slice(rows.stop - stored, rows.stop)
                nc.sync.dma_start(out=out_rows[:, pair, P * tt : P * (tt + 1)], in_=result[tt][:, pair, :])

        def output(tt, tags, skips_first=False):
            per_bank = PACK // len(tags)
            result[tt] = sb.tile([P, PACK, P], F32, name="result%d" % tt, align_bytes=64)
            parts = []
            for number, tag in enumerate(tags):
                bank = ps.tile([P, per_bank, P], F32, name="y%d_%d" % (tt, number), tag=tag)
                rows = range(per_bank * number, per_bank * (number + 1))
                skip_passes(bank, tt, rows)
                if skips_first:
                    parts.append((bank, rows))
                else:
                    second_passes(bank, tt, rows)
            for bank, rows in parts:
                second_passes(bank, tt, rows)

        def round_result(tt, parts):
            width = P // parts
            rounded[tt] = []
            for part in range(parts):
                piece = sb.tile([P, PACK * width], BF16, name="rounded%d_%d" % (tt, part), align_bytes=64)
                nc.vector.tensor_copy(
                    out=piece[:].rearrange("p (g i j) -> p g j i", j=PACK, i=4),
                    in_=result[tt][:, :, width * part : width * (part + 1)].rearrange("p j (g i) -> p g j i", i=4),
                )
                rounded[tt].append(piece)

        def hand_on(tt):
            width = P // len(rounded[tt])
            for part, piece in enumerate(rounded[tt]):
                nc.vector.quantize_mx(
                    out=out_w[:, P * tt + width * part : P * tt + width * (part + 1)].bitcast(FP8X4),
                    scales=out_s[:, P * tt + width * part : P * tt + width * (part + 1)],
                    in_=piece[:],
                )
            if tt % 2:
                pair = slice(P * (tt - 1), P * (tt + 1))
                nc.sync.dma_start(out=out_words[:, pair], in_=out_w[:, pair])

        larger(0)
        larger(1)
        larger(2)
        turn(0)
        turn(1)
        deal_b()
        quantize_hid(0)
        quantize_hid(1)
        larger(3)
        output(0, ["high0", "high1"], skips_first=True)
        turn(2)
        turn(3)
        round_result(0, 1)
        quantize_hid(2)
        hand_on(0)
        quantize_hid(3)
        output(1, ["high2", "low0"])
        round_result(1, 1)
        hand_on(1)
        output(2, ["high3", "low1"])
        round_result(2, 1)
        hand_on(2)
        output(3, ["high0", "high1", "low2", "low3"])
        round_result(3, 2)
        hand_on(3)

        for quad in range(QUADS):
            engine = nc.sync if quad == 3 else nc.scalar
            engine.dma_start(
                out=out_2[0, 4 * quad : 4 * quad + 4, :].bitcast(I32),
                in_=out_s[32 * quad : 32 * quad + 4, :].bitcast(I32),
            )
